import numpy as np
import ml_dtypes


def mxq(x, axis, fmt="e4m3"):
    dtype, down = {"e4m3": (ml_dtypes.float8_e4m3fn, 7), "e5m2": (ml_dtypes.float8_e5m2, 14)}[fmt]
    v = np.moveaxis(np.asarray(x, np.float32).astype(ml_dtypes.bfloat16).astype(np.float64), axis, -1)
    blocks = v.reshape(v.shape[:-1] + (-1, 32))
    amax = np.abs(blocks).max(-1, keepdims=True)
    byte = np.maximum(np.where(amax > 0, np.frexp(amax)[1] - 1 + 127, 0) - down, 1)
    scale = np.exp2(byte - 127.0)
    codes = (blocks / scale).astype(np.float32).astype(dtype).astype(np.float64)
    return np.moveaxis((codes * scale).reshape(v.shape), -1, axis)


WIDE = False


def mx_kscale(k):
    if not WIDE:
        return np.ones(k)
    levels = np.array([30, -30])
    if k % 512:
        return np.exp2(np.random.permutation(np.resize(levels, k // 32))).repeat(32)
    a = np.empty((k // 512, 16))
    for p in range(k // 512):
        a[p, :8] = np.random.permutation(np.resize(levels, 8))
        for g in range(8):
            far = levels[np.abs(levels - a[p, g]) >= 10]
            a[p, g + 8] = far[np.random.randint(len(far))]
    return np.exp2(a.ravel()).repeat(32)


def f64(x):
    return np.asarray(x).astype(np.float64)


def striped(idx):
    return np.tile(np.asarray(idx).reshape(-1, 16).T, (8, 1)).astype(np.uint16)


def unstriped(offs):
    return offs[:16].T.reshape(-1).astype(np.int64)


E2M1 = np.array([0.0, 0.5, 1.0, 1.5, 2.0, 3.0, 4.0, 6.0, -0.0, -0.5, -1.0, -1.5, -2.0, -3.0, -4.0, -6.0])


def pack_weight(w, fmt):
    k, n = w.shape
    w = f64(np.asarray(w, np.float32).astype(ml_dtypes.bfloat16)).reshape(k // 32, 32, n)
    amax = np.abs(w).max(1)
    if fmt in ("e4m3", "e5m2"):
        byte = np.frexp(amax)[1] - 1 + 127 - (7 if fmt == "e4m3" else 14)
    else:
        mant, ex = np.frexp(amax / 6.0)
        byte = np.where(mant > 0.5, ex, ex - 1) + 127
    byte = np.clip(np.where(amax > 0, byte, 1), 1, 254)
    scaled = (w * np.exp2(127.0 - byte)[:, None, :]).reshape(k, n).astype(np.float32)
    by_word = np.ascontiguousarray(scaled.reshape(k // 512, 128, 4, n).transpose(0, 1, 3, 2))
    if fmt in ("e4m3", "e5m2"):
        words = by_word.astype(ml_dtypes.float8_e4m3fn if fmt == "e4m3" else ml_dtypes.float8_e5m2).view(np.uint8)
    else:
        c = by_word.astype(ml_dtypes.float4_e2m1fn).view(np.uint8) & 0xF
        words = (c[..., 0::2] | (c[..., 1::2] << 4)).reshape(k // 512, 128, 2 * n)
    return np.ascontiguousarray(words), np.ascontiguousarray(byte.astype(np.uint8).reshape(k // 512, 16, n))


def unpack_weight(words, scales, fmt):
    g, _, n = scales.shape
    words = np.ascontiguousarray(words).reshape(g, 128, n, -1)
    if fmt in ("e4m3", "e5m2"):
        vals = words.view(ml_dtypes.float8_e4m3fn if fmt == "e4m3" else ml_dtypes.float8_e5m2).astype(np.float64)
    else:
        nib = np.empty((g, 128, n, 4), np.uint8)
        nib[..., 0::2] = words & 0xF
        nib[..., 1::2] = words >> 4
        vals = E2M1[nib]
    vals = vals * np.repeat(np.exp2(scales.astype(np.float64) - 127.0), 8, axis=1)[..., None]
    return vals.transpose(0, 1, 3, 2).reshape(g * 512, n)


K, T, J, I, R, C, Q = 512, 512, 256, 256, 512, 512, 512


def setup_inputs():
    n = np.random.standard_normal
    idx = np.random.permutation(T)[:J]
    idx2 = np.random.permutation(T)[:I]
    idx3 = np.random.permutation(C)[:I]
    idx4 = np.random.permutation(Q)[:I]
    fk = mx_kscale(K)
    fr = mx_kscale(R)
    xtp = pack_weight(n((K, T)) / fk[:, None], "e5m2")
    wap = pack_weight(n((K, R)) * 0.5 / np.sqrt(K) * fk[:, None] * fr, "e4m3")
    wbp = pack_weight(n((K, R)) * 1 / np.sqrt(K) * fk[:, None] / fr, "e2m1")
    return {
        "xt_words": xtp[0],
        "xt_scales": xtp[1],
        "wa_words": wap[0],
        "wa_scales": wap[1],
        "wb_words": wbp[0],
        "wb_scales": wbp[1],
        "tf": (n((R, C))).astype(np.float32),
        "tv": (1.0 * n((J, Q))).astype(np.float32),
        "offs": striped(idx),
        "offs2": striped(idx2),
        "offs3": striped(idx3),
        "offs4": striped(idx4),
    }


def reference(xt_words, xt_scales, wa_words, wa_scales, wb_words, wb_scales, tf, tv, offs, offs2, offs3, offs4):
    idx = unstriped(offs)
    idx2 = unstriped(offs2)
    idx3 = unstriped(offs3)
    idx4 = unstriped(offs4)
    xtu = unpack_weight(xt_words, xt_scales, "e5m2")
    wau = unpack_weight(wa_words, wa_scales, "e4m3")
    wbu = unpack_weight(wb_words, wb_scales, "e2m1")
    xtidxg = xtu[:, idx]
    za = wau.T @ xtidxg
    ya1 = np.pad(za, ((0, 0), (1, 0)))[:, :J]
    ha = za - 0.6 * ya1
    xtidx2g = xtu[:, idx2]
    zb = wbu.T @ xtidx2g
    hb = zb * f64(tf)[:, idx3]
    haq = mxq(ha, 0, "e5m2")
    hbq = mxq(hb, 0, "e4m3")
    a0 = haq.T @ hbq
    y = np.tanh(0.04 * a0) * f64(tv)[:, idx4]
    return y

@@ -1,0 +1,197 @@
+from contextlib import ExitStack
+
+import concourse.mybir as mybir
+
+K, T, J, I, R = 512, 512, 256, 256, 512
+FLOPS = 2 * K * R * J + 2 * K * R * I + 2 * R * J * I
+
+F32 = mybir.dt.float32
+BF16 = mybir.dt.bfloat16
+I32 = mybir.dt.int32
+U32 = mybir.dt.uint32
+U16 = mybir.dt.uint16
+U8 = mybir.dt.uint8
+E4M3 = mybir.dt.float8_e4m3fn_x4
+E5M2 = mybir.dt.float8_e5m2_x4
+E2M1 = mybir.dt.float4_e2m1fn_x4
+ACT = mybir.ActivationFunctionType
+ALU = mybir.AluOpType
+
+P = 128
+PACK = 4
+HALF = 128
+LAG = 0.6
+TANH_SCALE = 0.04
+
+
+def tile_list_meet_lagged_timestable_tabled_kernel(
+    tc, xt_words, xt_scales, wa_words, wa_scales, wb_words, wb_scales, tf, tv, offs, offs2, offs3, offs4, out
+):
+    nc = tc.nc
+    with ExitStack() as ctx:
+        sb = ctx.enter_context(tc.tile_pool(name="sb", bufs=1))
+        ps = ctx.enter_context(tc.psum_pool(name="ps", bufs=1))
+
+        def tile(name, shape, dtype):
+            return sb.tile(shape, dtype, name=name, align_bytes=64)
+
+        def load_list(name, src):
+            lst = tile(name, [P, 16], U16)
+            nc.sync.dma_start(lst[:], src)
+            return lst
+
+        def load_scales(name, src, queues):
+            plane = tile(name, [P, 512], U8)
+            for q in range(4):
+                rows = src[0][4 * q : 4 * q + 4, :].bitcast(I32)
+                queues[q].dma_start(
+                    plane[32 * q : 32 * q + 32, :].bitcast(I32),
+                    rows.unsqueeze(0).broadcast_to([8, 4, 128]),
+                )
+            return plane
+
+        def load_words(name, src, words):
+            dst = tile(name, [P, words], U32)
+            nc.sync.dma_start(dst[:].bitcast(I32), src.bitcast(I32))
+            return dst
+
+        tf_rows = tf.rearrange("(g t e) c -> t g e c", t=PACK, e=8)
+
+        def load_tf(t):
+            dst = tile("tf%d" % t, [P, 512], F32)
+            nc.sync.dma_start(dst[:], tf_rows[t])
+            return dst
+
+        def load_tv(h):
+            dst = tile("tv%d" % h, [P, 512], F32)
+            nc.sync.dma_start(dst[:], tv[h * HALF : (h + 1) * HALF, :])
+            return dst
+
+        list_a = load_list("list_a", offs)
+        x_scales = load_scales("x_scales", xt_scales, [nc.scalar] * 4)
+        x_words = load_words("x_words", xt_words[0].rearrange("p n t -> p (n t)"), T)
+        wa_raw = load_words("wa_raw", wa_words[0].rearrange("p n t -> p (n t)"), R)
+        tf_tiles = [load_tf(0)]
+        wa_scales_raw = load_scales("wa_scales_raw", wa_scales, [nc.sync] * 4)
+        list_b = load_list("list_b", offs2)
+        list_f = load_list("list_f", offs3)
+        tf_tiles.extend([load_tf(1), load_tf(2), load_tf(3)])
+        wb_raw = load_words("wb_raw", wb_words[0], R // 2)
+        wb_scales_raw = load_scales("wb_scales_raw", wb_scales, [nc.sync] * 4)
+        list_v = load_list("list_v", offs4)
+        tv_rows = tile("tv_rows", [P, 2, 512], F32)
+        nc.sync.dma_start(tv_rows[:], tv.rearrange("(h p) q -> p h q", p=P))
+
+        def deal(name, raw, bytes_per_column, copy, word):
+            dealt = tile(name, [P, R * bytes_per_column], U8)
+            run = 8 * bytes_per_column // 4
+            copy(
+                dealt[:].bitcast(word).rearrange("p (t g e) -> p t g e", t=PACK, e=run),
+                raw[:].bitcast(word).rearrange("p (g t e) -> p t g e", t=PACK, e=run),
+            )
+            return dealt
+
+        def gather_tokens(name, lst):
+            words = tile(name + "_words", [P, 256], U32)
+            scales = tile(name + "_scales", [P, 256], U8)
+            nc.vector.tensor_copy(words[:], x_words[:].indirect(lst[:]))
+            nc.vector.tensor_copy(scales[:], x_scales[:].indirect(lst[:]))
+            return words, scales
+
+        def first_stage(name, w, w_scales, fmt, bytes_per_column, x, x_sc, h):
+            bank = ps.tile([P, PACK, HALF], F32, name=name)
+            cols = slice(h * HALF, (h + 1) * HALF)
+            for t in range(PACK):
+                nc.tensor.matmul_mx(
+                    out=bank[:, t, :],
+                    lhsT=w[:, t * P * bytes_per_column : (t + 1) * P * bytes_per_column].bitcast(fmt),
+                    lhsT_scale=w_scales[:, t * P : (t + 1) * P],
+                    rhs=x[:, cols].bitcast(E5M2),
+                    rhs_scale=x_sc[:, cols],
+                    start=True,
+                    stop=True,
+                )
+            return bank
+
+        def quantise(name, values, fmt):
+            words = tile(name + "_words", [P, HALF], U32)
+            scales = tile(name + "_scales", [P, HALF], U8)
+            nc.vector.quantize_mx(out=words[:].bitcast(fmt), scales=scales[:], in_=values[:])
+            return words, scales
+
+        za = tile("za", [P, (J + 1) * PACK], F32)
+        nc.gpsimd.memset(za[:, 0:PACK], 0.0)
+
+        wa = deal("wa", wa_raw, 4, nc.scalar.copy, U32)
+        wa_sc = deal("wa_sc", wa_scales_raw, 1, nc.scalar.copy, U32)
+        xa, xa_sc = gather_tokens("xa", list_a)
+        xb, xb_sc = gather_tokens("xb", list_b)
+
+        tf_listed = tile("tf_listed", [P, PACK, I], F32)
+
+        def gather_tf_scalar(t):
+            nc.scalar.activation(tf_listed[:, t, :], tf_tiles[t][:].indirect(list_f[:]), ACT.Copy)
+
+        def gather_tf_vector(t):
+            nc.vector.tensor_copy(tf_listed[:, t, :], tf_tiles[t][:].indirect(list_f[:]))
+
+        gather_tf_vector(0)
+        ha = []
+        for h in range(2):
+            bank = first_stage("za_bank%d" % h, wa, wa_sc, E4M3, 4, xa, xa_sc, h)
+            lo = h * HALF * PACK
+            nc.scalar.copy(
+                za[:, lo + PACK : lo + PACK + HALF * PACK].rearrange("p (j t) -> p j t", t=PACK),
+                bank[:].rearrange("p t j -> p j t"),
+            )
+            ha.append(tile("ha%d" % h, [P, HALF * PACK], BF16))
+            nc.vector.scalar_tensor_tensor(
+                out=ha[h][:],
+                in0=za[:, lo : lo + HALF * PACK],
+                scalar=-LAG,
+                in1=za[:, lo + PACK : lo + PACK + HALF * PACK],
+                op0=ALU.mult,
+                op1=ALU.add,
+            )
+        for t in range(1, PACK):
+            gather_tf_scalar(t)
+        wb = deal("wb", wb_raw, 2, nc.vector.tensor_copy, I32)
+        wb_sc = deal("wb_sc", wb_scales_raw, 1, nc.vector.tensor_copy, I32)
+        ha_q = [quantise("ha_q%d" % h, ha[h], E5M2) for h in range(2)]
+
+        tv_listed = tile("tv_listed", [P, 2, I], F32)
+        for h in range(2):
+            nc.scalar.activation(tv_listed[:, h, :], tv_rows[:, h, :].indirect(list_v[:]), ACT.Copy)
+
+        out_rows = out.rearrange("(h p) i -> p h i", p=P)
+        hb = []
+        for g in range(2):
+            cols = slice(g * HALF, (g + 1) * HALF)
+            bank = first_stage("zb_bank%d" % g, wb, wb_sc, E2M1, 2, xb, xb_sc, g)
+            hb.append(tile("hb%d" % g, [P, HALF * PACK], BF16))
+            nc.vector.tensor_tensor(
+                out=hb[g][:].rearrange("p (c i t) -> p c t i", i=4, t=PACK),
+                in0=bank[:].rearrange("p t (c i) -> p c t i", i=4),
+                in1=tf_listed[:, :, cols].rearrange("p t (c i) -> p c t i", i=4),
+                op=ALU.mult,
+            )
+        hb_q = [quantise("hb_q%d" % g, hb[g], E4M3) for g in range(2)]
+        for g in range(2):
+            cols = slice(g * HALF, (g + 1) * HALF)
+            hb_words, hb_scales = hb_q[g]
+            scores = ps.tile([P, 2, HALF], F32, name="scores%d" % g)
+            for h in range(2):
+                nc.tensor.matmul_mx(
+                    out=scores[:, h, :],
+                    lhsT=ha_q[h][0][:].bitcast(E5M2),
+                    lhsT_scale=ha_q[h][1][:],
+                    rhs=hb_words[:].bitcast(E4M3),
+                    rhs_scale=hb_scales[:],
+                    start=True,
+                    stop=True,
+                )
+            squashed = tile("squashed%d" % g, [P, 2, HALF], F32)
+            nc.scalar.activation(squashed[:], scores[:], ACT.Tanh, scale=TANH_SCALE)
+            result = tile("result%d" % g, [P, 2, HALF], F32)
+            nc.vector.tensor_tensor(out=result[:], in0=squashed[:], in1=tv_listed[:, :, cols], op=ALU.mult)
+            nc.sync.dma_start(out_rows[:, :, cols], result[:])

@@ -40,15 +40,16 @@ def tile_list_meet_lagged_timestable_tabled_kernel(
             nc.sync.dma_start(lst[:], src)
             return lst
 
-        def load_scales(name, src, queues):
+        def zeroed_plane(name):
             plane = tile(name, [P, 512], U8)
-            for q in range(4):
-                rows = src[0][4 * q : 4 * q + 4, :].bitcast(I32)
-                queues[q].dma_start(
-                    plane[32 * q : 32 * q + 32, :].bitcast(I32),
-                    rows.unsqueeze(0).broadcast_to([8, 4, 128]),
-                )
+            nc.vector.memset(plane[:].bitcast(I32), 0)
             return plane
+
+        def load_scale_rows(plane, src, queue):
+            for q in range(4):
+                queue.dma_start(
+                    plane[32 * q : 32 * q + 4, :].bitcast(I32), src[0][4 * q : 4 * q + 4, :].bitcast(I32)
+                )
 
         def load_words(name, src, words):
             dst = tile(name, [P, words], U32)
@@ -67,20 +68,31 @@ def tile_list_meet_lagged_timestable_tabled_kernel(
             nc.sync.dma_start(dst[:], tv[h * HALF : (h + 1) * HALF, :])
             return dst
 
+        wa_scales_raw = zeroed_plane("wa_scales_raw")
+        wb_scales_raw = zeroed_plane("wb_scales_raw")
+        x_scales = zeroed_plane("x_scales")
+        x_scale_rows = tile("x_scale_rows", [P, 512], U8)
+
         list_a = load_list("list_a", offs)
-        x_scales = load_scales("x_scales", xt_scales, [nc.scalar] * 4)
-        x_words = load_words("x_words", xt_words[0].rearrange("p n t -> p (n t)"), T)
-        wa_raw = load_words("wa_raw", wa_words[0].rearrange("p n t -> p (n t)"), R)
-        tf_tiles = [load_tf(0)]
-        wa_scales_raw = load_scales("wa_scales_raw", wa_scales, [nc.sync] * 4)
         list_b = load_list("list_b", offs2)
+        load_scale_rows(x_scale_rows, xt_scales, nc.sync)
+        wa_raw = load_words("wa_raw", wa_words[0].rearrange("p n t -> p (n t)"), R)
+        x_words = load_words("x_words", xt_words[0].rearrange("p n t -> p (n t)"), T)
+        load_scale_rows(wa_scales_raw, wa_scales, nc.sync)
+        tf_tiles = [load_tf(0)]
         list_f = load_list("list_f", offs3)
-        tf_tiles.extend([load_tf(1), load_tf(2), load_tf(3)])
+        tf_tiles.append(load_tf(1))
+        tf_tiles.append(load_tf(2))
+        tf_tiles.append(load_tf(3))
         wb_raw = load_words("wb_raw", wb_words[0], R // 2)
-        wb_scales_raw = load_scales("wb_scales_raw", wb_scales, [nc.sync] * 4)
+        load_scale_rows(wb_scales_raw, wb_scales, nc.sync)
         list_v = load_list("list_v", offs4)
         tv_rows = tile("tv_rows", [P, 2, 512], F32)
         nc.sync.dma_start(tv_rows[:], tv.rearrange("(h p) q -> p h q", p=P))
+
+        for q in range(4):
+            rows = slice(32 * q, 32 * q + 4)
+            nc.vector.tensor_copy(x_scales[rows, :].bitcast(I32), x_scale_rows[rows, :].bitcast(I32))
 
         def deal(name, raw, bytes_per_column, copy, word):
             dealt = tile(name, [P, R * bytes_per_column], U8)
@@ -91,10 +103,14 @@ def tile_list_meet_lagged_timestable_tabled_kernel(
             )
             return dealt
 
-        def gather_tokens(name, lst):
+        def gather_tokens(name, lst, pieces):
             words = tile(name + "_words", [P, 256], U32)
             scales = tile(name + "_scales", [P, 256], U8)
-            nc.vector.tensor_copy(words[:], x_words[:].indirect(lst[:]))
+            for h in range(pieces):
+                n = 256 // pieces
+                nc.vector.tensor_copy(
+                    words[:, h * n : (h + 1) * n], x_words[:].indirect(lst[:, h * n // 16 : (h + 1) * n // 16])
+                )
             nc.vector.tensor_copy(scales[:], x_scales[:].indirect(lst[:]))
             return words, scales
 
@@ -119,15 +135,17 @@ def tile_list_meet_lagged_timestable_tabled_kernel(
             nc.vector.quantize_mx(out=words[:].bitcast(fmt), scales=scales[:], in_=values[:])
             return words, scales
 
-        za = tile("za", [P, (J + 1) * PACK], F32)
+        shared = tile("shared", [P, (PACK + 2) * I + PACK], F32)
+        tf_listed = shared[:, 0 : PACK * I].rearrange("p (t i) -> p t i", t=PACK)
+        tv_listed = shared[:, PACK * I : (PACK + 2) * I].rearrange("p (h i) -> p h i", h=2)
+        za = shared[:, 2 * I :]
         nc.gpsimd.memset(za[:, 0:PACK], 0.0)
 
         wa = deal("wa", wa_raw, 4, nc.scalar.copy, U32)
         wa_sc = deal("wa_sc", wa_scales_raw, 1, nc.scalar.copy, U32)
-        xa, xa_sc = gather_tokens("xa", list_a)
-        xb, xb_sc = gather_tokens("xb", list_b)
+        xa, xa_sc = gather_tokens("xa", list_a, 2)
+        xb, xb_sc = gather_tokens("xb", list_b, 1)
 
-        tf_listed = tile("tf_listed", [P, PACK, I], F32)
 
         def gather_tf_scalar(t):
             nc.scalar.activation(tf_listed[:, t, :], tf_tiles[t][:].indirect(list_f[:]), ACT.Copy)
@@ -135,7 +153,8 @@ def tile_list_meet_lagged_timestable_tabled_kernel(
         def gather_tf_vector(t):
             nc.vector.tensor_copy(tf_listed[:, t, :], tf_tiles[t][:].indirect(list_f[:]))
 
-        gather_tf_vector(0)
+        gather_tf_scalar(0)
+        gather_tf_vector(1)
         ha = []
         for h in range(2):
             bank = first_stage("za_bank%d" % h, wa, wa_sc, E4M3, 4, xa, xa_sc, h)
@@ -153,13 +172,18 @@ def tile_list_meet_lagged_timestable_tabled_kernel(
                 op0=ALU.mult,
                 op1=ALU.add,
             )
-        for t in range(1, PACK):
-            gather_tf_scalar(t)
-        wb = deal("wb", wb_raw, 2, nc.vector.tensor_copy, I32)
-        wb_sc = deal("wb_sc", wb_scales_raw, 1, nc.vector.tensor_copy, I32)
+            if h == 0:
+                wb = deal("wb", wb_raw, 2, nc.gpsimd.tensor_copy, I32)
+                wb_sc = deal("wb_sc", wb_scales_raw, 1, nc.gpsimd.tensor_copy, I32)
+        for g in range(2):
+            for t in range(2, PACK):
+                nc.scalar.activation(
+                    tf_listed[:, t, g * HALF : (g + 1) * HALF],
+                    tf_tiles[t][:].indirect(list_f[:, g * HALF // 16 : (g + 1) * HALF // 16]),
+                    ACT.Copy,
+                )
         ha_q = [quantise("ha_q%d" % h, ha[h], E5M2) for h in range(2)]
 
-        tv_listed = tile("tv_listed", [P, 2, I], F32)
         for h in range(2):
             nc.scalar.activation(tv_listed[:, h, :], tv_rows[:, h, :].indirect(list_v[:]), ACT.Copy)
 
@@ -179,10 +203,11 @@ def tile_list_meet_lagged_timestable_tabled_kernel(
         for g in range(2):
             cols = slice(g * HALF, (g + 1) * HALF)
             hb_words, hb_scales = hb_q[g]
-            scores = ps.tile([P, 2, HALF], F32, name="scores%d" % g)
+            result = tile("result%d" % g, [P, 2, HALF], F32)
             for h in range(2):
+                scores = ps.tile([P, HALF], F32, name="scores%d%d" % (g, h))
                 nc.tensor.matmul_mx(
-                    out=scores[:, h, :],
+                    out=scores[:],
                     lhsT=ha_q[h][0][:].bitcast(E5M2),
                     lhsT_scale=ha_q[h][1][:],
                     rhs=hb_words[:].bitcast(E4M3),
@@ -190,8 +215,7 @@ def tile_list_meet_lagged_timestable_tabled_kernel(
                     start=True,
                     stop=True,
                 )
-            squashed = tile("squashed%d" % g, [P, 2, HALF], F32)
-            nc.scalar.activation(squashed[:], scores[:], ACT.Tanh, scale=TANH_SCALE)
-            result = tile("result%d" % g, [P, 2, HALF], F32)
-            nc.vector.tensor_tensor(out=result[:], in0=squashed[:], in1=tv_listed[:, :, cols], op=ALU.mult)
+                squashed = tile("squashed%d%d" % (g, h), [P, HALF], F32)
+                nc.scalar.activation(squashed[:], scores[:], ACT.Tanh, scale=TANH_SCALE)
+                nc.vector.tensor_tensor(out=result[:, h, :], in0=squashed[:], in1=tv_listed[:, h, cols], op=ALU.mult)
             nc.sync.dma_start(out_rows[:, :, cols], result[:])

@@ -194,9 +194,9 @@ def tile_list_meet_lagged_timestable_tabled_kernel(
             bank = first_stage("zb_bank%d" % g, wb, wb_sc, E2M1, 2, xb, xb_sc, g)
             hb.append(tile("hb%d" % g, [P, HALF * PACK], BF16))
             nc.vector.tensor_tensor(
-                out=hb[g][:].rearrange("p (c i t) -> p c t i", i=4, t=PACK),
-                in0=bank[:].rearrange("p t (c i) -> p c t i", i=4),
-                in1=tf_listed[:, :, cols].rearrange("p t (c i) -> p c t i", i=4),
+                out=hb[g][:].rearrange("p (c i t) -> p c t i", i=2, t=PACK),
+                in0=bank[:].rearrange("p t (c i) -> p c t i", i=2),
+                in1=tf_listed[:, :, cols].rearrange("p t (c i) -> p c t i", i=2),
                 op=ALU.mult,
             )
         hb_q = [quantise("hb_q%d" % g, hb[g], E4M3) for g in range(2)]

from contextlib import ExitStack

import concourse.mybir as mybir

K, T, J, I, R = 512, 512, 256, 256, 512
FLOPS = 2 * K * R * J + 2 * K * R * I + 2 * R * J * I

F32 = mybir.dt.float32
BF16 = mybir.dt.bfloat16
I32 = mybir.dt.int32
U32 = mybir.dt.uint32
U16 = mybir.dt.uint16
U8 = mybir.dt.uint8
E4M3 = mybir.dt.float8_e4m3fn_x4
E5M2 = mybir.dt.float8_e5m2_x4
E2M1 = mybir.dt.float4_e2m1fn_x4
ACT = mybir.ActivationFunctionType
ALU = mybir.AluOpType

P = 128
PACK = 4
HALF = 128
LAG = 0.6
TANH_SCALE = 0.04


def tile_list_meet_lagged_timestable_tabled_kernel(
    tc, xt_words, xt_scales, wa_words, wa_scales, wb_words, wb_scales, tf, tv, offs, offs2, offs3, offs4, out
):
    nc = tc.nc
    with ExitStack() as ctx:
        sb = ctx.enter_context(tc.tile_pool(name="sb", bufs=1))
        ps = ctx.enter_context(tc.psum_pool(name="ps", bufs=1))

        def tile(name, shape, dtype):
            return sb.tile(shape, dtype, name=name, align_bytes=64)

        def load_list(name, src):
            lst = tile(name, [P, 16], U16)
            nc.sync.dma_start(lst[:], src)
            return lst

        def zeroed_plane(name):
            plane = tile(name, [P, 512], U8)
            nc.vector.memset(plane[:].bitcast(I32), 0)
            return plane

        def load_scale_rows(plane, src, queue):
            for q in range(4):
                queue.dma_start(
                    plane[32 * q : 32 * q + 4, :].bitcast(I32), src[0][4 * q : 4 * q + 4, :].bitcast(I32)
                )

        def load_words(name, src, words):
            dst = tile(name, [P, words], U32)
            nc.sync.dma_start(dst[:].bitcast(I32), src.bitcast(I32))
            return dst

        tf_rows = tf.rearrange("(g t e) c -> t g e c", t=PACK, e=8)

        def load_tf(t):
            dst = tile("tf%d" % t, [P, 512], F32)
            nc.sync.dma_start(dst[:], tf_rows[t])
            return dst

        def load_tv(h):
            dst = tile("tv%d" % h, [P, 512], F32)
            nc.sync.dma_start(dst[:], tv[h * HALF : (h + 1) * HALF, :])
            return dst

        wa_scales_raw = zeroed_plane("wa_scales_raw")
        wb_scales_raw = zeroed_plane("wb_scales_raw")
        x_scales = zeroed_plane("x_scales")
        x_scale_rows = tile("x_scale_rows", [P, 512], U8)

        list_a = load_list("list_a", offs)
        list_b = load_list("list_b", offs2)
        load_scale_rows(x_scale_rows, xt_scales, nc.sync)
        wa_raw = load_words("wa_raw", wa_words[0].rearrange("p n t -> p (n t)"), R)
        x_words = load_words("x_words", xt_words[0].rearrange("p n t -> p (n t)"), T)
        load_scale_rows(wa_scales_raw, wa_scales, nc.sync)
        tf_tiles = [load_tf(0)]
        list_f = load_list("list_f", offs3)
        tf_tiles.append(load_tf(1))
        tf_tiles.append(load_tf(2))
        tf_tiles.append(load_tf(3))
        wb_raw = load_words("wb_raw", wb_words[0], R // 2)
        load_scale_rows(wb_scales_raw, wb_scales, nc.sync)
        list_v = load_list("list_v", offs4)
        tv_rows = tile("tv_rows", [P, 2, 512], F32)
        nc.sync.dma_start(tv_rows[:], tv.rearrange("(h p) q -> p h q", p=P))

        for q in range(4):
            rows = slice(32 * q, 32 * q + 4)
            nc.vector.tensor_copy(x_scales[rows, :].bitcast(I32), x_scale_rows[rows, :].bitcast(I32))

        def deal(name, raw, bytes_per_column, copy, word):
            dealt = tile(name, [P, R * bytes_per_column], U8)
            run = 8 * bytes_per_column // 4
            copy(
                dealt[:].bitcast(word).rearrange("p (t g e) -> p t g e", t=PACK, e=run),
                raw[:].bitcast(word).rearrange("p (g t e) -> p t g e", t=PACK, e=run),
            )
            return dealt

        def gather_tokens(name, lst, pieces):
            words = tile(name + "_words", [P, 256], U32)
            scales = tile(name + "_scales", [P, 256], U8)
            for h in range(pieces):
                n = 256 // pieces
                nc.vector.tensor_copy(
                    words[:, h * n : (h + 1) * n], x_words[:].indirect(lst[:, h * n // 16 : (h + 1) * n // 16])
                )
            nc.vector.tensor_copy(scales[:], x_scales[:].indirect(lst[:]))
            return words, scales

        def first_stage(name, w, w_scales, fmt, bytes_per_column, x, x_sc, h):
            bank = ps.tile([P, PACK, HALF], F32, name=name)
            cols = slice(h * HALF, (h + 1) * HALF)
            for t in range(PACK):
                nc.tensor.matmul_mx(
                    out=bank[:, t, :],
                    lhsT=w[:, t * P * bytes_per_column : (t + 1) * P * bytes_per_column].bitcast(fmt),
                    lhsT_scale=w_scales[:, t * P : (t + 1) * P],
                    rhs=x[:, cols].bitcast(E5M2),
                    rhs_scale=x_sc[:, cols],
                    start=True,
                    stop=True,
                )
            return bank

        def quantise(name, values, fmt):
            words = tile(name + "_words", [P, HALF], U32)
            scales = tile(name + "_scales", [P, HALF], U8)
            nc.vector.quantize_mx(out=words[:].bitcast(fmt), scales=scales[:], in_=values[:])
            return words, scales

        shared = tile("shared", [P, (PACK + 2) * I + PACK], F32)
        tf_listed = shared[:, 0 : PACK * I].rearrange("p (t i) -> p t i", t=PACK)
        tv_listed = shared[:, PACK * I : (PACK + 2) * I].rearrange("p (h i) -> p h i", h=2)
        za = shared[:, 2 * I :]
        nc.gpsimd.memset(za[:, 0:PACK], 0.0)

        wa = deal("wa", wa_raw, 4, nc.scalar.copy, U32)
        wa_sc = deal("wa_sc", wa_scales_raw, 1, nc.scalar.copy, U32)
        xa, xa_sc = gather_tokens("xa", list_a, 2)
        xb, xb_sc = gather_tokens("xb", list_b, 1)


        def gather_tf_scalar(t):
            nc.scalar.activation(tf_listed[:, t, :], tf_tiles[t][:].indirect(list_f[:]), ACT.Copy)

        def gather_tf_vector(t):
            nc.vector.tensor_copy(tf_listed[:, t, :], tf_tiles[t][:].indirect(list_f[:]))

        gather_tf_scalar(0)
        gather_tf_vector(1)
        ha = []
        for h in range(2):
            bank = first_stage("za_bank%d" % h, wa, wa_sc, E4M3, 4, xa, xa_sc, h)
            lo = h * HALF * PACK
            nc.scalar.copy(
                za[:, lo + PACK : lo + PACK + HALF * PACK].rearrange("p (j t) -> p j t", t=PACK),
                bank[:].rearrange("p t j -> p j t"),
            )
            ha.append(tile("ha%d" % h, [P, HALF * PACK], BF16))
            nc.vector.scalar_tensor_tensor(
                out=ha[h][:],
                in0=za[:, lo : lo + HALF * PACK],
                scalar=-LAG,
                in1=za[:, lo + PACK : lo + PACK + HALF * PACK],
                op0=ALU.mult,
                op1=ALU.add,
            )
            if h == 0:
                wb = deal("wb", wb_raw, 2, nc.gpsimd.tensor_copy, I32)
                wb_sc = deal("wb_sc", wb_scales_raw, 1, nc.gpsimd.tensor_copy, I32)
        for g in range(2):
            for t in range(2, PACK):
                nc.scalar.activation(
                    tf_listed[:, t, g * HALF : (g + 1) * HALF],
                    tf_tiles[t][:].indirect(list_f[:, g * HALF // 16 : (g + 1) * HALF // 16]),
                    ACT.Copy,
                )
        ha_q = [quantise("ha_q%d" % h, ha[h], E5M2) for h in range(2)]

        for h in range(2):
            nc.scalar.activation(tv_listed[:, h, :], tv_rows[:, h, :].indirect(list_v[:]), ACT.Copy)

        out_rows = out.rearrange("(h p) i -> p h i", p=P)
        hb = []
        for g in range(2):
            cols = slice(g * HALF, (g + 1) * HALF)
            bank = first_stage("zb_bank%d" % g, wb, wb_sc, E2M1, 2, xb, xb_sc, g)
            hb.append(tile("hb%d" % g, [P, HALF * PACK], BF16))
            nc.vector.tensor_tensor(
                out=hb[g][:].rearrange("p (c i t) -> p c t i", i=2, t=PACK),
                in0=bank[:].rearrange("p t (c i) -> p c t i", i=2),
                in1=tf_listed[:, :, cols].rearrange("p t (c i) -> p c t i", i=2),
                op=ALU.mult,
            )
        hb_q = [quantise("hb_q%d" % g, hb[g], E4M3) for g in range(2)]
        for g in range(2):
            cols = slice(g * HALF, (g + 1) * HALF)
            hb_words, hb_scales = hb_q[g]
            result = tile("result%d" % g, [P, 2, HALF], F32)
            for h in range(2):
                scores = ps.tile([P, HALF], F32, name="scores%d%d" % (g, h))
                nc.tensor.matmul_mx(
                    out=scores[:],
                    lhsT=ha_q[h][0][:].bitcast(E5M2),
                    lhsT_scale=ha_q[h][1][:],
                    rhs=hb_words[:].bitcast(E4M3),
                    rhs_scale=hb_scales[:],
                    start=True,
                    stop=True,
                )
                squashed = tile("squashed%d%d" % (g, h), [P, HALF], F32)
                nc.scalar.activation(squashed[:], scores[:], ACT.Tanh, scale=TANH_SCALE)
                nc.vector.tensor_tensor(out=result[:, h, :], in0=squashed[:], in1=tv_listed[:, h, cols], op=ALU.mult)
            nc.sync.dma_start(out_rows[:, :, cols], result[:])
